import numpy as np
import ml_dtypes


def mxq(x, axis, fmt="e4m3"):
    dtype, down = {"e4m3": (ml_dtypes.float8_e4m3fn, 7), "e5m2": (ml_dtypes.float8_e5m2, 14)}[fmt]
    v = np.moveaxis(np.asarray(x, np.float32).astype(ml_dtypes.bfloat16).astype(np.float64), axis, -1)
    blocks = v.reshape(v.shape[:-1] + (-1, 32))
    amax = np.abs(blocks).max(-1, keepdims=True)
    byte = np.maximum(np.where(amax > 0, np.frexp(amax)[1] - 1 + 127, 0) - down, 1)
    scale = np.exp2(byte - 127.0)
    codes = (blocks / scale).astype(np.float32).astype(dtype).astype(np.float64)
    return np.moveaxis((codes * scale).reshape(v.shape), -1, axis)


WIDE = False


def mx_kscale(k):
    if not WIDE:
        return np.ones(k)
    levels = np.array([10, -10, 5, -5, 0])
    if k % 512:
        return np.exp2(np.random.permutation(np.resize(levels, k // 32))).repeat(32)
    a = np.empty((k // 512, 16))
    for p in range(k // 512):
        a[p, :8] = np.random.permutation(np.resize(levels, 8))
        for g in range(8):
            far = levels[np.abs(levels - a[p, g]) >= 10]
            a[p, g + 8] = far[np.random.randint(len(far))]
    return np.exp2(a.ravel()).repeat(32)


BF16 = ml_dtypes.bfloat16


def bf(x):
    return np.asarray(x, np.float32).astype(BF16)


def f64(x):
    return np.asarray(x).astype(np.float64)

def planes(Y):
    n, m = Y.shape
    b = f64(bf(Y)).reshape(n // 32, 32, m)
    amax = np.abs(b).max(1)
    byte = np.clip(np.where(amax > 0, np.frexp(amax)[1] - 1 + 127 - 7, 1), 1, 254)
    codes = (b * np.exp2(127.0 - byte)[:, None, :]).reshape(n, m).astype(np.float32).astype(ml_dtypes.float8_e4m3fn).view(np.uint8)
    words = codes.reshape(n // 512, 128, 4, m).transpose(0, 1, 3, 2)
    return np.ascontiguousarray(words), np.ascontiguousarray(byte.astype(np.uint8).reshape(n // 512, 16, m))


R, B, O = 4096, 1024, 512

OCC_LOW, OCC_HIGH = 0.2, 2.0
WEIGHT_SPREAD = 0.8


def setup_inputs():
    s = mx_kscale(B)
    ao = np.random.randn(R, B) * s[None, :]
    coeff = np.random.randn(B, O) / np.sqrt(B) / s[:, None]
    occ = np.random.uniform(OCC_LOW, OCC_HIGH, O)
    weight = np.exp(WEIGHT_SPREAD * np.random.randn(R))
    return {"ao": bf(ao), "coeff": bf(coeff), "occ": bf(occ), "weight": bf(weight)}


def reference(ao, coeff, occ, weight):
    a = mxq(f64(ao), 1, "e4m3")
    c = mxq(f64(coeff), 0, "e4m3")
    psi = a @ c
    density = psi * psi * f64(occ)[None, :]
    y = density * f64(weight)[:, None]
    Y = y.reshape(R, O)
    words, scales = planes(Y)
    return y, words, scales

@@ -1,0 +1,221 @@
+from contextlib import ExitStack
+
+import concourse.mybir as mybir
+from concourse.masks import make_identity
+
+R, B, O = 4096, 1024, 512
+FLOPS = 2 * R * B * O
+
+F32 = mybir.dt.float32
+BF16 = mybir.dt.bfloat16
+U32 = mybir.dt.uint32
+I32 = mybir.dt.int32
+U8 = mybir.dt.uint8
+FP8X4 = mybir.dt.float8_e4m3fn_x4
+ACT = mybir.ActivationFunctionType
+ALU = mybir.AluOpType
+
+P = 128
+PACK = 4
+GROUP = P * PACK
+GROUPS = R // GROUP
+PASSES = B // GROUP
+SUM_BANKS = 3
+POOL_COLS = 384
+EARLY_SCALE_GROUPS = 6
+
+
+def tile_weighted_orbital_densities_g2_kernel(tc, ao, coeff, occ, weight, out_0, out_1, out_2):
+    nc = tc.nc
+    with ExitStack() as ctx:
+        keep = ctx.enter_context(tc.tile_pool(name="keep", bufs=1))
+        psum = ctx.enter_context(tc.psum_pool(name="psum", bufs=1))
+        ctx.enter_context(tc.manual_schedule())
+
+        ident = keep.tile([P, P], F32, name="ident")
+        occ_bf = keep.tile([P, PACK], BF16, name="occ_bf")
+        occ_f32 = keep.tile([P, PACK], F32, name="occ_f32")
+        w_sb = keep.tile([P, GROUPS, PACK], BF16, name="w_sb")
+        c_raw = [keep.tile([P, PACK, O], BF16, name="c_raw%d" % s) for s in range(PASSES)]
+        c_packed = [keep.tile([P, O * PACK], BF16, name="c_packed%d" % s, align_bytes=64) for s in range(PASSES)]
+        c_codes = [keep.tile([P, O], U32, name="c_codes%d" % s, align_bytes=64) for s in range(PASSES)]
+        c_scales = [keep.tile([P, O], U8, name="c_scales%d" % s, align_bytes=64) for s in range(PASSES)]
+        a_raw = [keep.tile([P, PACK, B], BF16, name="a_raw%d" % g) for g in range(GROUPS)]
+        packed = [keep.tile([P, PACK * B], BF16, name="packed%d" % i, align_bytes=64) for i in range(2)]
+        a_codes = [keep.tile([P, PACK, PASSES * P], U32, name="a_codes%d" % i, align_bytes=64) for i in range(2)]
+        a_scales = [keep.tile([P, PACK, PASSES * P], U8, name="a_scales%d" % i, align_bytes=64) for i in range(2)]
+        squares = [keep.tile([P, PACK, O], F32, name="squares%d" % i) for i in range(2)]
+        y_f32 = [keep.tile([P, PACK, O], F32, name="y_f32_%d" % g) for g in range(GROUPS)]
+        y_codes = [keep.tile([P, O], U32, name="y_codes%d" % g, align_bytes=64) for g in range(GROUPS)]
+        y_scales = keep.tile([P, GROUPS, O], U8, name="y_scales", align_bytes=64)
+
+        turn_banks = [psum.tile([P, PASSES * 2, P], F32, name="turn%d" % t) for t in range(PACK)]
+        sum_banks = [psum.tile([P, O], F32, name="sum%d" % i) for i in range(SUM_BANKS)]
+        occ_bank = psum.tile([P, PACK, P], F32, name="occ_bank")
+
+        def ao_rows(g):
+            return ao[g * GROUP : (g + 1) * GROUP, :].rearrange("(p t) k -> p t k", t=PACK)
+
+        def load_ao(g, t0, t1):
+            nc.sync.dma_start(out=a_raw[g][:, t0:t1, :], in_=ao_rows(g)[:, t0:t1, :])
+
+        def load_coeff(s):
+            rows = coeff[s * GROUP : (s + 1) * GROUP, :]
+            nc.sync.dma_start(out=c_raw[s][:], in_=rows.rearrange("(p j) n -> p j n", j=PACK))
+
+        def pack_coeff(s):
+            nc.vector.tensor_copy(
+                out=c_packed[s][:].rearrange("p (c i j) -> p c j i", i=4, j=PACK),
+                in_=c_raw[s][:].rearrange("p j (c i) -> p c j i", i=4),
+            )
+
+        def quantize_coeff(s):
+            nc.vector.quantize_mx(out=c_codes[s][:].bitcast(FP8X4), scales=c_scales[s][:], in_=c_packed[s][:])
+
+        def turn_ao(g, t):
+            words = a_raw[g][:, t, :].bitcast(F32)
+            for s in range(PASSES):
+                for u in range(2):
+                    nc.tensor.transpose(
+                        turn_banks[t][:, 2 * s + u, :], words[:, 256 * s + u : 256 * (s + 1) : 2], ident[:]
+                    )
+            dst = packed[g % 2][:, t * B : (t + 1) * B].bitcast(F32)
+            nc.scalar.copy(
+                out=dst.rearrange("p (s r u) -> p s r u", s=PASSES, u=2),
+                in_=turn_banks[t][:].rearrange("p (s u) r -> p s r u", u=2),
+            )
+
+        def quantize_ao(g, t):
+            nc.vector.quantize_mx(
+                out=a_codes[g % 2][:, t, :].bitcast(FP8X4),
+                scales=a_scales[g % 2][:, t, :],
+                in_=packed[g % 2][:, t * B : (t + 1) * B],
+            )
+
+        def multiply(g, t):
+            bank = sum_banks[(PACK * g + t) % SUM_BANKS]
+            for s in range(PASSES):
+                cols = slice(s * P, (s + 1) * P)
+                nc.tensor.matmul_mx(
+                    out=bank[:],
+                    lhsT=a_codes[g % 2][:, t, cols].bitcast(FP8X4),
+                    lhsT_scale=a_scales[g % 2][:, t, cols],
+                    rhs=c_codes[s][:].bitcast(FP8X4),
+                    rhs_scale=c_scales[s][:],
+                    start=(s == 0),
+                    stop=(s == PASSES - 1),
+                )
+            nc.scalar.activation(out=squares[g % 2][:, t, :], in_=bank[:], func=ACT.Square)
+
+        def weigh(g, t):
+            nc.vector.scalar_tensor_tensor(
+                out=y_f32[g][:, t, :].rearrange("p (n j) -> p n j", j=PACK),
+                in0=squares[g % 2][:, t, :].rearrange("p (n j) -> p n j", j=PACK),
+                scalar=w_sb[:, g, t : t + 1],
+                in1=occ_bank[:].rearrange("p j n -> p n j"),
+                op0=ALU.mult,
+                op1=ALU.mult,
+            )
+
+        def y_packed(g):
+            return packed[(g + 1) % 2][:, 2 * B : 4 * B]
+
+        def y_views(g, m0, m1):
+            dst = y_packed(g)[:, PACK * m0 : PACK * m1].rearrange("p (m t) -> p m t", t=PACK)
+            src = y_f32[g][:, :, m0:m1].rearrange("p t m -> p m t")
+            return dst, src
+
+        def pack_y_pool(g, m0, m1):
+            dst, src = y_views(g, m0, m1)
+            nc.gpsimd.tensor_scalar(out=dst, in0=src, scalar1=1.0, scalar2=0.0, op0=ALU.mult, op1=ALU.add)
+
+        def pack_y_vector(g, m0, m1):
+            dst, src = y_views(g, m0, m1)
+            nc.vector.tensor_copy(out=dst, in_=src)
+
+        def pack_y_scalar(g, m0, m1):
+            dst, src = y_views(g, m0, m1)
+            nc.scalar.copy(out=dst, in_=src)
+
+        def quantize_y(g, m0, m1):
+            nc.vector.quantize_mx(
+                out=y_codes[g][:, m0:m1].bitcast(FP8X4),
+                scales=y_scales[:, g, m0:m1],
+                in_=y_packed(g)[:, PACK * m0 : PACK * m1],
+            )
+
+        def store_y(g, t0, t1):
+            rows = out_0[g * GROUP : (g + 1) * GROUP, :].rearrange("(p t) m -> p t m", t=PACK)
+            nc.sync.dma_start(out=rows[:, t0:t1, :], in_=y_f32[g][:, t0:t1, :])
+
+        def store_words(g, m0, m1):
+            words = out_1[g].rearrange("p m t -> p (m t)").bitcast(I32)
+            nc.sync.dma_start(out=words[:, m0:m1], in_=y_codes[g][:, m0:m1].bitcast(I32))
+
+        def store_scales(g0, g1, queue):
+            for q in range(4):
+                rows = out_2[g0:g1, 4 * q : 4 * q + 4, :].rearrange("g r m -> r g m")
+                queue.dma_start(out=rows.bitcast(I32), in_=y_scales[32 * q : 32 * q + 4, g0:g1, :].bitcast(I32))
+
+        nc.scalar.dma_start(out=occ_bf[:], in_=occ.rearrange("(p j) -> p j", j=PACK))
+        nc.scalar.dma_start(out=w_sb[:], in_=weight.rearrange("(g p t) -> p g t", p=P, t=PACK))
+        load_coeff(0)
+        load_ao(0, 0, 1)
+        load_coeff(1)
+        load_ao(0, 1, 2)
+        load_ao(0, 2, 4)
+        for g in range(1, GROUPS):
+            load_ao(g, 0, 2)
+            load_ao(g, 2, 4)
+
+        make_identity(nc, ident[:])
+        nc.scalar.activation(out=occ_f32[:], in_=occ_bf[:], func=ACT.Identity)
+
+        pack_coeff(0)
+        turn_ao(0, 0)
+        for j in range(PACK):
+            nc.tensor.transpose(occ_bank[:, j, :], occ_f32[:, j : j + 1].to_broadcast([P, P]), ident[:])
+        quantize_coeff(0)
+        pack_coeff(1)
+        quantize_ao(0, 0)
+        quantize_coeff(1)
+        for t in range(1, PACK):
+            turn_ao(0, t)
+            quantize_ao(0, t)
+
+        last = GROUPS - 1
+        for g in range(GROUPS):
+            if g > 0:
+                pack_y_pool(g - 1, 0, POOL_COLS)
+            for t in range(PACK):
+                multiply(g, t)
+                weigh(g, t)
+                if g == last:
+                    store_y(g, t, t + 1)
+            if g < last:
+                store_y(g, 0, PACK)
+                for t in range(PACK):
+                    turn_ao(g + 1, t)
+                quantize_ao(g + 1, 0)
+                if g > 0:
+                    pack_y_vector(g - 1, POOL_COLS, O)
+                quantize_ao(g + 1, 1)
+                if g > 0:
+                    quantize_y(g - 1, 0, O)
+                    store_words(g - 1, 0, O)
+                quantize_ao(g + 1, 2)
+                quantize_ao(g + 1, 3)
+                if g == EARLY_SCALE_GROUPS:
+                    store_scales(0, EARLY_SCALE_GROUPS, nc.sync)
+
+        half = O // 2
+        pack_y_scalar(last - 1, POOL_COLS, O)
+        pack_y_vector(last, 0, half)
+        pack_y_scalar(last, half, O)
+        quantize_y(last - 1, 0, O)
+        store_words(last - 1, 0, O)
+        quantize_y(last, 0, half)
+        store_words(last, 0, half)
+        quantize_y(last, half, O)
+        store_words(last, half, O)
+        store_scales(EARLY_SCALE_GROUPS, GROUPS, nc.scalar)

@@ -20,8 +20,9 @@ PACK = 4
 GROUP = P * PACK
 GROUPS = R // GROUP
 PASSES = B // GROUP
-SUM_BANKS = 3
-POOL_COLS = 384
+SUM_BANKS = 4
+HALF = O // 2
+SCALAR_COLS = 64
 EARLY_SCALE_GROUPS = 6
 
 
@@ -35,6 +36,7 @@ def tile_weighted_orbital_densities_g2_kernel(tc, ao, coeff, occ, weight, out_0,
         ident = keep.tile([P, P], F32, name="ident")
         occ_bf = keep.tile([P, PACK], BF16, name="occ_bf")
         occ_f32 = keep.tile([P, PACK], F32, name="occ_f32")
+        occ_row = keep.tile([P, O], F32, name="occ_row")
         w_sb = keep.tile([P, GROUPS, PACK], BF16, name="w_sb")
         c_raw = [keep.tile([P, PACK, O], BF16, name="c_raw%d" % s) for s in range(PASSES)]
         c_packed = [keep.tile([P, O * PACK], BF16, name="c_packed%d" % s, align_bytes=64) for s in range(PASSES)]
@@ -42,6 +44,7 @@ def tile_weighted_orbital_densities_g2_kernel(tc, ao, coeff, occ, weight, out_0,
         c_scales = [keep.tile([P, O], U8, name="c_scales%d" % s, align_bytes=64) for s in range(PASSES)]
         a_raw = [keep.tile([P, PACK, B], BF16, name="a_raw%d" % g) for g in range(GROUPS)]
         packed = [keep.tile([P, PACK * B], BF16, name="packed%d" % i, align_bytes=64) for i in range(2)]
+        y_bf = [keep.tile([P, PACK * O], BF16, name="y_bf%d" % i, align_bytes=64) for i in range(2)]
         a_codes = [keep.tile([P, PACK, PASSES * P], U32, name="a_codes%d" % i, align_bytes=64) for i in range(2)]
         a_scales = [keep.tile([P, PACK, PASSES * P], U8, name="a_scales%d" % i, align_bytes=64) for i in range(2)]
         squares = [keep.tile([P, PACK, O], F32, name="squares%d" % i) for i in range(2)]
@@ -51,7 +54,6 @@ def tile_weighted_orbital_densities_g2_kernel(tc, ao, coeff, occ, weight, out_0,
 
         turn_banks = [psum.tile([P, PASSES * 2, P], F32, name="turn%d" % t) for t in range(PACK)]
         sum_banks = [psum.tile([P, O], F32, name="sum%d" % i) for i in range(SUM_BANKS)]
-        occ_bank = psum.tile([P, PACK, P], F32, name="occ_bank")
 
         def ao_rows(g):
             return ao[g * GROUP : (g + 1) * GROUP, :].rearrange("(p t) k -> p t k", t=PACK)
@@ -85,49 +87,45 @@ def tile_weighted_orbital_densities_g2_kernel(tc, ao, coeff, occ, weight, out_0,
                 in_=turn_banks[t][:].rearrange("p (s u) r -> p s r u", u=2),
             )
 
-        def quantize_ao(g, t):
+        def quantize_ao(h):
+            g, t0 = h // 2, 2 * (h % 2)
             nc.vector.quantize_mx(
-                out=a_codes[g % 2][:, t, :].bitcast(FP8X4),
-                scales=a_scales[g % 2][:, t, :],
-                in_=packed[g % 2][:, t * B : (t + 1) * B],
+                out=a_codes[g % 2][:, t0 : t0 + 2, :].rearrange("p t c -> p (t c)").bitcast(FP8X4),
+                scales=a_scales[g % 2][:, t0 : t0 + 2, :].rearrange("p t c -> p (t c)"),
+                in_=packed[g % 2][:, t0 * B : (t0 + 2) * B],
             )
 
-        def multiply(g, t):
-            bank = sum_banks[(PACK * g + t) % SUM_BANKS]
+        def multiply(g, t, m0, m1, bank):
             for s in range(PASSES):
                 cols = slice(s * P, (s + 1) * P)
                 nc.tensor.matmul_mx(
-                    out=bank[:],
+                    out=bank[:, 0 : m1 - m0],
                     lhsT=a_codes[g % 2][:, t, cols].bitcast(FP8X4),
                     lhsT_scale=a_scales[g % 2][:, t, cols],
-                    rhs=c_codes[s][:].bitcast(FP8X4),
-                    rhs_scale=c_scales[s][:],
+                    rhs=c_codes[s][:, m0:m1].bitcast(FP8X4),
+                    rhs_scale=c_scales[s][:, m0:m1],
                     start=(s == 0),
                     stop=(s == PASSES - 1),
                 )
-            nc.scalar.activation(out=squares[g % 2][:, t, :], in_=bank[:], func=ACT.Square)
+            nc.scalar.activation(out=squares[g % 2][:, t, m0:m1], in_=bank[:, 0 : m1 - m0], func=ACT.Square)
 
-        def weigh(g, t):
+        def weigh(g, t, m0, m1):
             nc.vector.scalar_tensor_tensor(
-                out=y_f32[g][:, t, :].rearrange("p (n j) -> p n j", j=PACK),
-                in0=squares[g % 2][:, t, :].rearrange("p (n j) -> p n j", j=PACK),
+                out=y_f32[g][:, t, m0:m1],
+                in0=squares[g % 2][:, t, m0:m1],
                 scalar=w_sb[:, g, t : t + 1],
-                in1=occ_bank[:].rearrange("p j n -> p n j"),
+                in1=occ_row[:, m0:m1],
                 op0=ALU.mult,
                 op1=ALU.mult,
             )
 
         def y_packed(g):
-            return packed[(g + 1) % 2][:, 2 * B : 4 * B]
+            return y_bf[g % 2][:]
 
         def y_views(g, m0, m1):
-            dst = y_packed(g)[:, PACK * m0 : PACK * m1].rearrange("p (m t) -> p m t", t=PACK)
-            src = y_f32[g][:, :, m0:m1].rearrange("p t m -> p m t")
+            dst = y_packed(g)[:, PACK * m0 : PACK * m1].rearrange("p (c i t) -> p c t i", i=4, t=PACK)
+            src = y_f32[g][:, :, m0:m1].rearrange("p t (c i) -> p c t i", i=4)
             return dst, src
-
-        def pack_y_pool(g, m0, m1):
-            dst, src = y_views(g, m0, m1)
-            nc.gpsimd.tensor_scalar(out=dst, in0=src, scalar1=1.0, scalar2=0.0, op0=ALU.mult, op1=ALU.add)
 
         def pack_y_vector(g, m0, m1):
             dst, src = y_views(g, m0, m1)
@@ -152,13 +150,12 @@ def tile_weighted_orbital_densities_g2_kernel(tc, ao, coeff, occ, weight, out_0,
             words = out_1[g].rearrange("p m t -> p (m t)").bitcast(I32)
             nc.sync.dma_start(out=words[:, m0:m1], in_=y_codes[g][:, m0:m1].bitcast(I32))
 
-        def store_scales(g0, g1, queue):
+        def store_scales(g0, g1, queues):
             for q in range(4):
                 rows = out_2[g0:g1, 4 * q : 4 * q + 4, :].rearrange("g r m -> r g m")
-                queue.dma_start(out=rows.bitcast(I32), in_=y_scales[32 * q : 32 * q + 4, g0:g1, :].bitcast(I32))
+                queues[q % 2].dma_start(out=rows.bitcast(I32), in_=y_scales[32 * q : 32 * q + 4, g0:g1, :].bitcast(I32))
 
         nc.scalar.dma_start(out=occ_bf[:], in_=occ.rearrange("(p j) -> p j", j=PACK))
-        nc.scalar.dma_start(out=w_sb[:], in_=weight.rearrange("(g p t) -> p g t", p=P, t=PACK))
         load_coeff(0)
         load_ao(0, 0, 1)
         load_coeff(1)
@@ -170,52 +167,67 @@ def tile_weighted_orbital_densities_g2_kernel(tc, ao, coeff, occ, weight, out_0,
 
         make_identity(nc, ident[:])
         nc.scalar.activation(out=occ_f32[:], in_=occ_bf[:], func=ACT.Identity)
+        nc.scalar.dma_start(out=w_sb[:], in_=weight.rearrange("(g p t) -> p g t", p=P, t=PACK))
 
         pack_coeff(0)
         turn_ao(0, 0)
+        occ_bank = sum_banks[SUM_BANKS - 1][:].rearrange("p (j n) -> p j n", j=PACK)
         for j in range(PACK):
             nc.tensor.transpose(occ_bank[:, j, :], occ_f32[:, j : j + 1].to_broadcast([P, P]), ident[:])
+        nc.scalar.copy(out=occ_row[:].rearrange("p (n j) -> p n j", j=PACK), in_=occ_bank.rearrange("p j n -> p n j"))
         quantize_coeff(0)
         pack_coeff(1)
-        quantize_ao(0, 0)
+        turn_ao(0, 1)
+        quantize_ao(0)
         quantize_coeff(1)
-        for t in range(1, PACK):
-            turn_ao(0, t)
-            quantize_ao(0, t)
+        turn_ao(0, 2)
+        turn_ao(0, 3)
 
         last = GROUPS - 1
-        for g in range(GROUPS):
+        for h in range(2 * last):
+            g, j = h // 2, h % 2
+            t0 = 2 * j
+            m0, m1 = j * HALF, (j + 1) * HALF
+            multiply(g, t0, 0, O, sum_banks[t0][:])
+            multiply(g, t0 + 1, 0, O, sum_banks[t0 + 1][:])
             if g > 0:
-                pack_y_pool(g - 1, 0, POOL_COLS)
-            for t in range(PACK):
-                multiply(g, t)
-                weigh(g, t)
-                if g == last:
-                    store_y(g, t, t + 1)
-            if g < last:
-                store_y(g, 0, PACK)
-                for t in range(PACK):
-                    turn_ao(g + 1, t)
-                quantize_ao(g + 1, 0)
-                if g > 0:
-                    pack_y_vector(g - 1, POOL_COLS, O)
-                quantize_ao(g + 1, 1)
-                if g > 0:
-                    quantize_y(g - 1, 0, O)
+                pack_y_scalar(g - 1, m1 - SCALAR_COLS, m1)
+            quantize_ao(h + 1)
+            weigh(g, t0, 0, O)
+            if g > 0:
+                pack_y_vector(g - 1, m0, m1 - SCALAR_COLS)
+            weigh(g, t0 + 1, 0, O)
+            store_y(g, t0, t0 + 2)
+            if g > 0:
+                quantize_y(g - 1, m0, m1)
+                if j == 1:
                     store_words(g - 1, 0, O)
-                quantize_ao(g + 1, 2)
-                quantize_ao(g + 1, 3)
-                if g == EARLY_SCALE_GROUPS:
-                    store_scales(0, EARLY_SCALE_GROUPS, nc.sync)
+            turn_ao(g + 1, t0)
+            turn_ao(g + 1, t0 + 1)
+        store_scales(0, EARLY_SCALE_GROUPS, [nc.sync, nc.sync])
 
-        half = O // 2
-        pack_y_scalar(last - 1, POOL_COLS, O)
-        pack_y_vector(last, 0, half)
-        pack_y_scalar(last, half, O)
-        quantize_y(last - 1, 0, O)
+        multiply(last, 0, 0, O, sum_banks[0][:])
+        multiply(last, 1, 0, O, sum_banks[1][:])
+        quantize_ao(2 * last + 1)
+        pack_y_vector(last - 1, HALF, O)
+        weigh(last, 0, 0, O)
+        weigh(last, 1, 0, O)
+        store_y(last, 0, 2)
+        quantize_y(last - 1, HALF, O)
+        spare = [turn_banks[i][:].rearrange("p a r -> p (a r)") for i in range(2)]
+        banks = [sum_banks[2][:], sum_banks[3][:], spare[0], spare[1]]
+        for j in range(2):
+            for t in range(2, PACK):
+                multiply(last, t, j * HALF, (j + 1) * HALF, banks[2 * j + t - 2])
+                weigh(last, t, j * HALF, (j + 1) * HALF)
+        store_y(last, 2, PACK)
+        pack_y_scalar(last - 1, 0, HALF)
+        pack_y_vector(last, 0, HALF + HALF // 2)
+        pack_y_scalar(last, HALF + HALF // 2, O)
+        quantize_y(last - 1, 0, HALF)
         store_words(last - 1, 0, O)
-        quantize_y(last, 0, half)
-        store_words(last, 0, half)
-        quantize_y(last, half, O)
-        store_words(last, half, O)
-        store_scales(EARLY_SCALE_GROUPS, GROUPS, nc.scalar)
+        quantize_y(last, 0, HALF)
+        store_words(last, 0, HALF)
+        quantize_y(last, HALF, O)
+        store_words(last, HALF, O)
+        store_scales(EARLY_SCALE_GROUPS, GROUPS, [nc.scalar, nc.sync])

@@ -20,9 +20,10 @@ PACK = 4
 GROUP = P * PACK
 GROUPS = R // GROUP
 PASSES = B // GROUP
-SUM_BANKS = 4
+SUM_BANKS = 3
 HALF = O // 2
-SCALAR_COLS = 64
+POOL_COLS = 416
+POOL_COLS_LATE = 352
 EARLY_SCALE_GROUPS = 6
 
 
@@ -36,15 +37,13 @@ def tile_weighted_orbital_densities_g2_kernel(tc, ao, coeff, occ, weight, out_0,
         ident = keep.tile([P, P], F32, name="ident")
         occ_bf = keep.tile([P, PACK], BF16, name="occ_bf")
         occ_f32 = keep.tile([P, PACK], F32, name="occ_f32")
-        occ_row = keep.tile([P, O], F32, name="occ_row")
         w_sb = keep.tile([P, GROUPS, PACK], BF16, name="w_sb")
         c_raw = [keep.tile([P, PACK, O], BF16, name="c_raw%d" % s) for s in range(PASSES)]
         c_packed = [keep.tile([P, O * PACK], BF16, name="c_packed%d" % s, align_bytes=64) for s in range(PASSES)]
         c_codes = [keep.tile([P, O], U32, name="c_codes%d" % s, align_bytes=64) for s in range(PASSES)]
         c_scales = [keep.tile([P, O], U8, name="c_scales%d" % s, align_bytes=64) for s in range(PASSES)]
         a_raw = [keep.tile([P, PACK, B], BF16, name="a_raw%d" % g) for g in range(GROUPS)]
-        packed = [keep.tile([P, PACK * B], BF16, name="packed%d" % i, align_bytes=64) for i in range(2)]
-        y_bf = [keep.tile([P, PACK * O], BF16, name="y_bf%d" % i, align_bytes=64) for i in range(2)]
+        packed = [keep.tile([P, 2 * B], BF16, name="packed%d" % i, align_bytes=64) for i in range(4)]
         a_codes = [keep.tile([P, PACK, PASSES * P], U32, name="a_codes%d" % i, align_bytes=64) for i in range(2)]
         a_scales = [keep.tile([P, PACK, PASSES * P], U8, name="a_scales%d" % i, align_bytes=64) for i in range(2)]
         squares = [keep.tile([P, PACK, O], F32, name="squares%d" % i) for i in range(2)]
@@ -54,6 +53,7 @@ def tile_weighted_orbital_densities_g2_kernel(tc, ao, coeff, occ, weight, out_0,
 
         turn_banks = [psum.tile([P, PASSES * 2, P], F32, name="turn%d" % t) for t in range(PACK)]
         sum_banks = [psum.tile([P, O], F32, name="sum%d" % i) for i in range(SUM_BANKS)]
+        occ_bank = psum.tile([P, PACK, P], F32, name="occ_bank")
 
         def ao_rows(g):
             return ao[g * GROUP : (g + 1) * GROUP, :].rearrange("(p t) k -> p t k", t=PACK)
@@ -65,10 +65,10 @@ def tile_weighted_orbital_densities_g2_kernel(tc, ao, coeff, occ, weight, out_0,
             rows = coeff[s * GROUP : (s + 1) * GROUP, :]
             nc.sync.dma_start(out=c_raw[s][:], in_=rows.rearrange("(p j) n -> p j n", j=PACK))
 
-        def pack_coeff(s):
-            nc.vector.tensor_copy(
-                out=c_packed[s][:].rearrange("p (c i j) -> p c j i", i=4, j=PACK),
-                in_=c_raw[s][:].rearrange("p j (c i) -> p c j i", i=4),
+        def pack_coeff(s, m0, m1, copy):
+            copy(
+                out=c_packed[s][:, PACK * m0 : PACK * m1].rearrange("p (c i j) -> p c j i", i=4, j=PACK),
+                in_=c_raw[s][:, :, m0:m1].rearrange("p j (c i) -> p c j i", i=4),
             )
 
         def quantize_coeff(s):
@@ -81,18 +81,18 @@ def tile_weighted_orbital_densities_g2_kernel(tc, ao, coeff, occ, weight, out_0,
                     nc.tensor.transpose(
                         turn_banks[t][:, 2 * s + u, :], words[:, 256 * s + u : 256 * (s + 1) : 2], ident[:]
                     )
-            dst = packed[g % 2][:, t * B : (t + 1) * B].bitcast(F32)
+            dst = packed[(2 * g + t // 2) % 4][:, (t % 2) * B : (t % 2 + 1) * B].bitcast(F32)
             nc.scalar.copy(
                 out=dst.rearrange("p (s r u) -> p s r u", s=PASSES, u=2),
                 in_=turn_banks[t][:].rearrange("p (s u) r -> p s r u", u=2),
             )
 
-        def quantize_ao(h):
+        def quantize_ao(h, v0=0, v1=2):
             g, t0 = h // 2, 2 * (h % 2)
             nc.vector.quantize_mx(
-                out=a_codes[g % 2][:, t0 : t0 + 2, :].rearrange("p t c -> p (t c)").bitcast(FP8X4),
-                scales=a_scales[g % 2][:, t0 : t0 + 2, :].rearrange("p t c -> p (t c)"),
-                in_=packed[g % 2][:, t0 * B : (t0 + 2) * B],
+                out=a_codes[g % 2][:, t0 + v0 : t0 + v1, :].rearrange("p t c -> p (t c)").bitcast(FP8X4),
+                scales=a_scales[g % 2][:, t0 + v0 : t0 + v1, :].rearrange("p t c -> p (t c)"),
+                in_=packed[h % 4][:, v0 * B : v1 * B],
             )
 
         def multiply(g, t, m0, m1, bank):
@@ -111,21 +111,26 @@ def tile_weighted_orbital_densities_g2_kernel(tc, ao, coeff, occ, weight, out_0,
 
         def weigh(g, t, m0, m1):
             nc.vector.scalar_tensor_tensor(
-                out=y_f32[g][:, t, m0:m1],
-                in0=squares[g % 2][:, t, m0:m1],
+                out=y_f32[g][:, t, m0:m1].rearrange("p (n j) -> p n j", j=PACK),
+                in0=squares[g % 2][:, t, m0:m1].rearrange("p (n j) -> p n j", j=PACK),
                 scalar=w_sb[:, g, t : t + 1],
-                in1=occ_row[:, m0:m1],
+                in1=occ_bank[:, :, m0 // PACK : m1 // PACK].rearrange("p j n -> p n j"),
                 op0=ALU.mult,
                 op1=ALU.mult,
             )
 
         def y_packed(g):
-            return y_bf[g % 2][:]
+            h = [4, 6, 8, 10, 12, 14, 14, 15][g]
+            return packed[h % 4][:]
 
         def y_views(g, m0, m1):
-            dst = y_packed(g)[:, PACK * m0 : PACK * m1].rearrange("p (c i t) -> p c t i", i=4, t=PACK)
-            src = y_f32[g][:, :, m0:m1].rearrange("p t (c i) -> p c t i", i=4)
+            dst = y_packed(g)[:, PACK * m0 : PACK * m1].rearrange("p (m t) -> p m t", t=PACK)
+            src = y_f32[g][:, :, m0:m1].rearrange("p t m -> p m t")
             return dst, src
+
+        def pack_y_pool(g, m0, m1):
+            dst, src = y_views(g, m0, m1)
+            nc.gpsimd.tensor_scalar(out=dst, in0=src, scalar1=1.0, scalar2=0.0, op0=ALU.mult, op1=ALU.add)
 
         def pack_y_vector(g, m0, m1):
             dst, src = y_views(g, m0, m1)
@@ -169,65 +174,79 @@ def tile_weighted_orbital_densities_g2_kernel(tc, ao, coeff, occ, weight, out_0,
         nc.scalar.activation(out=occ_f32[:], in_=occ_bf[:], func=ACT.Identity)
         nc.scalar.dma_start(out=w_sb[:], in_=weight.rearrange("(g p t) -> p g t", p=P, t=PACK))
 
-        pack_coeff(0)
-        turn_ao(0, 0)
-        occ_bank = sum_banks[SUM_BANKS - 1][:].rearrange("p (j n) -> p j n", j=PACK)
-        for j in range(PACK):
-            nc.tensor.transpose(occ_bank[:, j, :], occ_f32[:, j : j + 1].to_broadcast([P, P]), ident[:])
-        nc.scalar.copy(out=occ_row[:].rearrange("p (n j) -> p n j", j=PACK), in_=occ_bank.rearrange("p j n -> p n j"))
-        quantize_coeff(0)
-        pack_coeff(1)
-        turn_ao(0, 1)
-        quantize_ao(0)
-        quantize_coeff(1)
-        turn_ao(0, 2)
-        turn_ao(0, 3)
+        def turn_half(h):
+            for t in range(2 * (h % 2), 2 * (h % 2) + 2):
+                turn_ao(h // 2, t)
 
-        last = GROUPS - 1
-        for h in range(2 * last):
-            g, j = h // 2, h % 2
-            t0 = 2 * j
-            m0, m1 = j * HALF, (j + 1) * HALF
-            multiply(g, t0, 0, O, sum_banks[t0][:])
-            multiply(g, t0 + 1, 0, O, sum_banks[t0 + 1][:])
-            if g > 0:
-                pack_y_scalar(g - 1, m1 - SCALAR_COLS, m1)
-            quantize_ao(h + 1)
+        def multiply_unit(g, t):
+            multiply(g, t, 0, O, sum_banks[(PACK * g + t) % SUM_BANKS][:])
+
+        def weigh_half(h):
+            g, t0 = h // 2, 2 * (h % 2)
             weigh(g, t0, 0, O)
-            if g > 0:
-                pack_y_vector(g - 1, m0, m1 - SCALAR_COLS)
             weigh(g, t0 + 1, 0, O)
             store_y(g, t0, t0 + 2)
+
+        def multiply_half(h):
+            g, t0 = h // 2, 2 * (h % 2)
+            multiply_unit(g, t0)
+            multiply_unit(g, t0 + 1)
+            weigh_half(h)
+
+        pack_coeff(0, 0, O, nc.vector.tensor_copy)
+        turn_ao(0, 0)
+        for j in range(PACK):
+            nc.tensor.transpose(occ_bank[:, j, :], occ_f32[:, j : j + 1].to_broadcast([P, P]), ident[:])
+        quantize_coeff(0)
+        quantize_ao(0, 0, 1)
+        pack_coeff(1, 0, HALF, nc.vector.tensor_copy)
+        pack_coeff(1, HALF, O, nc.scalar.copy)
+        turn_ao(0, 1)
+        quantize_coeff(1)
+        quantize_ao(0, 1, 2)
+        turn_half(1)
+        quantize_ao(1)
+        multiply_unit(0, 0)
+        turn_half(2)
+        multiply_unit(0, 1)
+        weigh_half(0)
+        quantize_ao(2)
+        turn_half(3)
+
+        last = GROUPS - 1
+        for g in range(last):
             if g > 0:
-                quantize_y(g - 1, m0, m1)
-                if j == 1:
-                    store_words(g - 1, 0, O)
-            turn_ao(g + 1, t0)
-            turn_ao(g + 1, t0 + 1)
+                pack_y_pool(g - 1, 0, POOL_COLS)
+                multiply_half(2 * g)
+                turn_half(2 * g + 3)
+            multiply_half(2 * g + 1)
+            if g < last - 1:
+                turn_half(2 * g + 4)
+            if g > 0:
+                pack_y_vector(g - 1, POOL_COLS, O)
+            quantize_ao(2 * g + 3)
+            if g > 0:
+                quantize_y(g - 1, 0, O)
+                store_words(g - 1, 0, O)
+            if g < last - 1:
+                quantize_ao(2 * g + 4)
         store_scales(0, EARLY_SCALE_GROUPS, [nc.sync, nc.sync])
 
-        multiply(last, 0, 0, O, sum_banks[0][:])
-        multiply(last, 1, 0, O, sum_banks[1][:])
-        quantize_ao(2 * last + 1)
-        pack_y_vector(last - 1, HALF, O)
-        weigh(last, 0, 0, O)
-        weigh(last, 1, 0, O)
-        store_y(last, 0, 2)
-        quantize_y(last - 1, HALF, O)
-        spare = [turn_banks[i][:].rearrange("p a r -> p (a r)") for i in range(2)]
-        banks = [sum_banks[2][:], sum_banks[3][:], spare[0], spare[1]]
+        pack_y_pool(last - 1, 0, POOL_COLS_LATE)
+        multiply_half(2 * last)
+        spare = [turn_banks[i][:].rearrange("p a r -> p (a r)") for i in range(PACK)]
         for j in range(2):
             for t in range(2, PACK):
-                multiply(last, t, j * HALF, (j + 1) * HALF, banks[2 * j + t - 2])
+                multiply(last, t, j * HALF, (j + 1) * HALF, spare[2 * j + t - 2])
                 weigh(last, t, j * HALF, (j + 1) * HALF)
         store_y(last, 2, PACK)
-        pack_y_scalar(last - 1, 0, HALF)
-        pack_y_vector(last, 0, HALF + HALF // 2)
-        pack_y_scalar(last, HALF + HALF // 2, O)
-        quantize_y(last - 1, 0, HALF)
+        pack_y_scalar(last - 1, POOL_COLS_LATE, O)
+        pack_y_scalar(last, 0, HALF)
+        pack_y_vector(last, HALF, O)
+        quantize_y(last - 1, 0, O)
         store_words(last - 1, 0, O)
-        quantize_y(last, 0, HALF)
-        store_words(last, 0, HALF)
         quantize_y(last, HALF, O)
         store_words(last, HALF, O)
+        quantize_y(last, 0, HALF)
+        store_words(last, 0, HALF)
         store_scales(EARLY_SCALE_GROUPS, GROUPS, [nc.scalar, nc.sync])

@@ -22,8 +22,8 @@ GROUPS = R // GROUP
 PASSES = B // GROUP
 SUM_BANKS = 3
 HALF = O // 2
-POOL_COLS = 416
-POOL_COLS_LATE = 352
+POOL_COLS = 360
+POOL_COLS_LATE = 320
 EARLY_SCALE_GROUPS = 6
 
 
@@ -35,9 +35,8 @@ def tile_weighted_orbital_densities_g2_kernel(tc, ao, coeff, occ, weight, out_0,
         ctx.enter_context(tc.manual_schedule())
 
         ident = keep.tile([P, P], F32, name="ident")
-        occ_bf = keep.tile([P, PACK], BF16, name="occ_bf")
-        occ_f32 = keep.tile([P, PACK], F32, name="occ_f32")
-        w_sb = keep.tile([P, GROUPS, PACK], BF16, name="w_sb")
+        factor_rows = keep.tile([P, GROUP], BF16, name="factor_rows")
+        factors = keep.tile([P, GROUPS + 1, PACK], F32, name="factors")
         c_raw = [keep.tile([P, PACK, O], BF16, name="c_raw%d" % s) for s in range(PASSES)]
         c_packed = [keep.tile([P, O * PACK], BF16, name="c_packed%d" % s, align_bytes=64) for s in range(PASSES)]
         c_codes = [keep.tile([P, O], U32, name="c_codes%d" % s, align_bytes=64) for s in range(PASSES)]
@@ -113,7 +112,7 @@ def tile_weighted_orbital_densities_g2_kernel(tc, ao, coeff, occ, weight, out_0,
             nc.vector.scalar_tensor_tensor(
                 out=y_f32[g][:, t, m0:m1].rearrange("p (n j) -> p n j", j=PACK),
                 in0=squares[g % 2][:, t, m0:m1].rearrange("p (n j) -> p n j", j=PACK),
-                scalar=w_sb[:, g, t : t + 1],
+                scalar=factors[:, g, t : t + 1],
                 in1=occ_bank[:, :, m0 // PACK : m1 // PACK].rearrange("p j n -> p n j"),
                 op0=ALU.mult,
                 op1=ALU.mult,
@@ -160,19 +159,27 @@ def tile_weighted_orbital_densities_g2_kernel(tc, ao, coeff, occ, weight, out_0,
                 rows = out_2[g0:g1, 4 * q : 4 * q + 4, :].rearrange("g r m -> r g m")
                 queues[q % 2].dma_start(out=rows.bitcast(I32), in_=y_scales[32 * q : 32 * q + 4, g0:g1, :].bitcast(I32))
 
-        nc.scalar.dma_start(out=occ_bf[:], in_=occ.rearrange("(p j) -> p j", j=PACK))
+        nc.vector.memset(factor_rows[:], 0.0)
         load_coeff(0)
+        nc.sync.dma_start(out=factor_rows[0:GROUPS, :], in_=weight.rearrange("(g k) -> g k", g=GROUPS))
+        nc.sync.dma_start(out=factor_rows[GROUPS : GROUPS + 1, :], in_=occ.rearrange("(a k) -> a k", a=1))
         load_ao(0, 0, 1)
         load_coeff(1)
         load_ao(0, 1, 2)
         load_ao(0, 2, 4)
-        for g in range(1, GROUPS):
-            load_ao(g, 0, 2)
-            load_ao(g, 2, 4)
+        load_ao(1, 0, 2)
+        load_ao(1, 2, 4)
+        for g in range(2, GROUPS):
+            load_ao(g, 0, PACK)
 
         make_identity(nc, ident[:])
-        nc.scalar.activation(out=occ_f32[:], in_=occ_bf[:], func=ACT.Identity)
-        nc.scalar.dma_start(out=w_sb[:], in_=weight.rearrange("(g p t) -> p g t", p=P, t=PACK))
+        factor_words = factor_rows[:].bitcast(F32)
+        for u in range(2):
+            nc.tensor.transpose(sum_banks[0][:, u * P : (u + 1) * P], factor_words[:, u : 2 * P : 2], ident[:])
+        turned = sum_banks[0][:, 0 : 2 * P].bitcast(BF16).rearrange("p (u r e) -> p r u e", u=2, e=2)
+        nc.scalar.activation(
+            out=factors[:].rearrange("p r (u e) -> p r u e", u=2), in_=turned[:, 0 : GROUPS + 1], func=ACT.Identity
+        )
 
         def turn_half(h):
             for t in range(2 * (h % 2), 2 * (h % 2) + 2):
@@ -185,7 +192,10 @@ def tile_weighted_orbital_densities_g2_kernel(tc, ao, coeff, occ, weight, out_0,
             g, t0 = h // 2, 2 * (h % 2)
             weigh(g, t0, 0, O)
             weigh(g, t0 + 1, 0, O)
-            store_y(g, t0, t0 + 2)
+            if g >= GROUPS - 3:
+                store_y(g, t0, t0 + 2)
+            elif t0 == 2:
+                store_y(g, 0, PACK)
 
         def multiply_half(h):
             g, t0 = h // 2, 2 * (h % 2)
@@ -196,7 +206,7 @@ def tile_weighted_orbital_densities_g2_kernel(tc, ao, coeff, occ, weight, out_0,
         pack_coeff(0, 0, O, nc.vector.tensor_copy)
         turn_ao(0, 0)
         for j in range(PACK):
-            nc.tensor.transpose(occ_bank[:, j, :], occ_f32[:, j : j + 1].to_broadcast([P, P]), ident[:])
+            nc.tensor.transpose(occ_bank[:, j, :], factors[:, GROUPS, j : j + 1].to_broadcast([P, P]), ident[:])
         quantize_coeff(0)
         quantize_ao(0, 0, 1)
         pack_coeff(1, 0, HALF, nc.vector.tensor_copy)
@@ -222,7 +232,9 @@ def tile_weighted_orbital_densities_g2_kernel(tc, ao, coeff, occ, weight, out_0,
             multiply_half(2 * g + 1)
             if g < last - 1:
                 turn_half(2 * g + 4)
-            if g > 0:
+            if g == last - 1:
+                pack_y_scalar(g - 1, POOL_COLS, O)
+            elif g > 0:
                 pack_y_vector(g - 1, POOL_COLS, O)
             quantize_ao(2 * g + 3)
             if g > 0:

from contextlib import ExitStack

import concourse.mybir as mybir
from concourse.masks import make_identity

R, B, O = 4096, 1024, 512
FLOPS = 2 * R * B * O

F32 = mybir.dt.float32
BF16 = mybir.dt.bfloat16
U32 = mybir.dt.uint32
I32 = mybir.dt.int32
U8 = mybir.dt.uint8
FP8X4 = mybir.dt.float8_e4m3fn_x4
ACT = mybir.ActivationFunctionType
ALU = mybir.AluOpType

P = 128
PACK = 4
GROUP = P * PACK
GROUPS = R // GROUP
PASSES = B // GROUP
SUM_BANKS = 3
HALF = O // 2
POOL_COLS = 360
POOL_COLS_LATE = 320
EARLY_SCALE_GROUPS = 6


def tile_weighted_orbital_densities_g2_kernel(tc, ao, coeff, occ, weight, out_0, out_1, out_2):
    nc = tc.nc
    with ExitStack() as ctx:
        keep = ctx.enter_context(tc.tile_pool(name="keep", bufs=1))
        psum = ctx.enter_context(tc.psum_pool(name="psum", bufs=1))
        ctx.enter_context(tc.manual_schedule())

        ident = keep.tile([P, P], F32, name="ident")
        factor_rows = keep.tile([P, GROUP], BF16, name="factor_rows")
        factors = keep.tile([P, GROUPS + 1, PACK], F32, name="factors")
        c_raw = [keep.tile([P, PACK, O], BF16, name="c_raw%d" % s) for s in range(PASSES)]
        c_packed = [keep.tile([P, O * PACK], BF16, name="c_packed%d" % s, align_bytes=64) for s in range(PASSES)]
        c_codes = [keep.tile([P, O], U32, name="c_codes%d" % s, align_bytes=64) for s in range(PASSES)]
        c_scales = [keep.tile([P, O], U8, name="c_scales%d" % s, align_bytes=64) for s in range(PASSES)]
        a_raw = [keep.tile([P, PACK, B], BF16, name="a_raw%d" % g) for g in range(GROUPS)]
        packed = [keep.tile([P, 2 * B], BF16, name="packed%d" % i, align_bytes=64) for i in range(4)]
        a_codes = [keep.tile([P, PACK, PASSES * P], U32, name="a_codes%d" % i, align_bytes=64) for i in range(2)]
        a_scales = [keep.tile([P, PACK, PASSES * P], U8, name="a_scales%d" % i, align_bytes=64) for i in range(2)]
        squares = [keep.tile([P, PACK, O], F32, name="squares%d" % i) for i in range(2)]
        y_f32 = [keep.tile([P, PACK, O], F32, name="y_f32_%d" % g) for g in range(GROUPS)]
        y_codes = [keep.tile([P, O], U32, name="y_codes%d" % g, align_bytes=64) for g in range(GROUPS)]
        y_scales = keep.tile([P, GROUPS, O], U8, name="y_scales", align_bytes=64)

        turn_banks = [psum.tile([P, PASSES * 2, P], F32, name="turn%d" % t) for t in range(PACK)]
        sum_banks = [psum.tile([P, O], F32, name="sum%d" % i) for i in range(SUM_BANKS)]
        occ_bank = psum.tile([P, PACK, P], F32, name="occ_bank")

        def ao_rows(g):
            return ao[g * GROUP : (g + 1) * GROUP, :].rearrange("(p t) k -> p t k", t=PACK)

        def load_ao(g, t0, t1):
            nc.sync.dma_start(out=a_raw[g][:, t0:t1, :], in_=ao_rows(g)[:, t0:t1, :])

        def load_coeff(s):
            rows = coeff[s * GROUP : (s + 1) * GROUP, :]
            nc.sync.dma_start(out=c_raw[s][:], in_=rows.rearrange("(p j) n -> p j n", j=PACK))

        def pack_coeff(s, m0, m1, copy):
            copy(
                out=c_packed[s][:, PACK * m0 : PACK * m1].rearrange("p (c i j) -> p c j i", i=4, j=PACK),
                in_=c_raw[s][:, :, m0:m1].rearrange("p j (c i) -> p c j i", i=4),
            )

        def quantize_coeff(s):
            nc.vector.quantize_mx(out=c_codes[s][:].bitcast(FP8X4), scales=c_scales[s][:], in_=c_packed[s][:])

        def turn_ao(g, t):
            words = a_raw[g][:, t, :].bitcast(F32)
            for s in range(PASSES):
                for u in range(2):
                    nc.tensor.transpose(
                        turn_banks[t][:, 2 * s + u, :], words[:, 256 * s + u : 256 * (s + 1) : 2], ident[:]
                    )
            dst = packed[(2 * g + t // 2) % 4][:, (t % 2) * B : (t % 2 + 1) * B].bitcast(F32)
            nc.scalar.copy(
                out=dst.rearrange("p (s r u) -> p s r u", s=PASSES, u=2),
                in_=turn_banks[t][:].rearrange("p (s u) r -> p s r u", u=2),
            )

        def quantize_ao(h, v0=0, v1=2):
            g, t0 = h // 2, 2 * (h % 2)
            nc.vector.quantize_mx(
                out=a_codes[g % 2][:, t0 + v0 : t0 + v1, :].rearrange("p t c -> p (t c)").bitcast(FP8X4),
                scales=a_scales[g % 2][:, t0 + v0 : t0 + v1, :].rearrange("p t c -> p (t c)"),
                in_=packed[h % 4][:, v0 * B : v1 * B],
            )

        def multiply(g, t, m0, m1, bank):
            for s in range(PASSES):
                cols = slice(s * P, (s + 1) * P)
                nc.tensor.matmul_mx(
                    out=bank[:, 0 : m1 - m0],
                    lhsT=a_codes[g % 2][:, t, cols].bitcast(FP8X4),
                    lhsT_scale=a_scales[g % 2][:, t, cols],
                    rhs=c_codes[s][:, m0:m1].bitcast(FP8X4),
                    rhs_scale=c_scales[s][:, m0:m1],
                    start=(s == 0),
                    stop=(s == PASSES - 1),
                )
            nc.scalar.activation(out=squares[g % 2][:, t, m0:m1], in_=bank[:, 0 : m1 - m0], func=ACT.Square)

        def weigh(g, t, m0, m1):
            nc.vector.scalar_tensor_tensor(
                out=y_f32[g][:, t, m0:m1].rearrange("p (n j) -> p n j", j=PACK),
                in0=squares[g % 2][:, t, m0:m1].rearrange("p (n j) -> p n j", j=PACK),
                scalar=factors[:, g, t : t + 1],
                in1=occ_bank[:, :, m0 // PACK : m1 // PACK].rearrange("p j n -> p n j"),
                op0=ALU.mult,
                op1=ALU.mult,
            )

        def y_packed(g):
            h = [4, 6, 8, 10, 12, 14, 14, 15][g]
            return packed[h % 4][:]

        def y_views(g, m0, m1):
            dst = y_packed(g)[:, PACK * m0 : PACK * m1].rearrange("p (m t) -> p m t", t=PACK)
            src = y_f32[g][:, :, m0:m1].rearrange("p t m -> p m t")
            return dst, src

        def pack_y_pool(g, m0, m1):
            dst, src = y_views(g, m0, m1)
            nc.gpsimd.tensor_scalar(out=dst, in0=src, scalar1=1.0, scalar2=0.0, op0=ALU.mult, op1=ALU.add)

        def pack_y_vector(g, m0, m1):
            dst, src = y_views(g, m0, m1)
            nc.vector.tensor_copy(out=dst, in_=src)

        def pack_y_scalar(g, m0, m1):
            dst, src = y_views(g, m0, m1)
            nc.scalar.copy(out=dst, in_=src)

        def quantize_y(g, m0, m1):
            nc.vector.quantize_mx(
                out=y_codes[g][:, m0:m1].bitcast(FP8X4),
                scales=y_scales[:, g, m0:m1],
                in_=y_packed(g)[:, PACK * m0 : PACK * m1],
            )

        def store_y(g, t0, t1):
            rows = out_0[g * GROUP : (g + 1) * GROUP, :].rearrange("(p t) m -> p t m", t=PACK)
            nc.sync.dma_start(out=rows[:, t0:t1, :], in_=y_f32[g][:, t0:t1, :])

        def store_words(g, m0, m1):
            words = out_1[g].rearrange("p m t -> p (m t)").bitcast(I32)
            nc.sync.dma_start(out=words[:, m0:m1], in_=y_codes[g][:, m0:m1].bitcast(I32))

        def store_scales(g0, g1, queues):
            for q in range(4):
                rows = out_2[g0:g1, 4 * q : 4 * q + 4, :].rearrange("g r m -> r g m")
                queues[q % 2].dma_start(out=rows.bitcast(I32), in_=y_scales[32 * q : 32 * q + 4, g0:g1, :].bitcast(I32))

        nc.vector.memset(factor_rows[:], 0.0)
        load_coeff(0)
        nc.sync.dma_start(out=factor_rows[0:GROUPS, :], in_=weight.rearrange("(g k) -> g k", g=GROUPS))
        nc.sync.dma_start(out=factor_rows[GROUPS : GROUPS + 1, :], in_=occ.rearrange("(a k) -> a k", a=1))
        load_ao(0, 0, 1)
        load_coeff(1)
        load_ao(0, 1, 2)
        load_ao(0, 2, 4)
        load_ao(1, 0, 2)
        load_ao(1, 2, 4)
        for g in range(2, GROUPS):
            load_ao(g, 0, PACK)

        make_identity(nc, ident[:])
        factor_words = factor_rows[:].bitcast(F32)
        for u in range(2):
            nc.tensor.transpose(sum_banks[0][:, u * P : (u + 1) * P], factor_words[:, u : 2 * P : 2], ident[:])
        turned = sum_banks[0][:, 0 : 2 * P].bitcast(BF16).rearrange("p (u r e) -> p r u e", u=2, e=2)
        nc.scalar.activation(
            out=factors[:].rearrange("p r (u e) -> p r u e", u=2), in_=turned[:, 0 : GROUPS + 1], func=ACT.Identity
        )

        def turn_half(h):
            for t in range(2 * (h % 2), 2 * (h % 2) + 2):
                turn_ao(h // 2, t)

        def multiply_unit(g, t):
            multiply(g, t, 0, O, sum_banks[(PACK * g + t) % SUM_BANKS][:])

        def weigh_half(h):
            g, t0 = h // 2, 2 * (h % 2)
            weigh(g, t0, 0, O)
            weigh(g, t0 + 1, 0, O)
            if g >= GROUPS - 3:
                store_y(g, t0, t0 + 2)
            elif t0 == 2:
                store_y(g, 0, PACK)

        def multiply_half(h):
            g, t0 = h // 2, 2 * (h % 2)
            multiply_unit(g, t0)
            multiply_unit(g, t0 + 1)
            weigh_half(h)

        pack_coeff(0, 0, O, nc.vector.tensor_copy)
        turn_ao(0, 0)
        for j in range(PACK):
            nc.tensor.transpose(occ_bank[:, j, :], factors[:, GROUPS, j : j + 1].to_broadcast([P, P]), ident[:])
        quantize_coeff(0)
        quantize_ao(0, 0, 1)
        pack_coeff(1, 0, HALF, nc.vector.tensor_copy)
        pack_coeff(1, HALF, O, nc.scalar.copy)
        turn_ao(0, 1)
        quantize_coeff(1)
        quantize_ao(0, 1, 2)
        turn_half(1)
        quantize_ao(1)
        multiply_unit(0, 0)
        turn_half(2)
        multiply_unit(0, 1)
        weigh_half(0)
        quantize_ao(2)
        turn_half(3)

        last = GROUPS - 1
        for g in range(last):
            if g > 0:
                pack_y_pool(g - 1, 0, POOL_COLS)
                multiply_half(2 * g)
                turn_half(2 * g + 3)
            multiply_half(2 * g + 1)
            if g < last - 1:
                turn_half(2 * g + 4)
            if g == last - 1:
                pack_y_scalar(g - 1, POOL_COLS, O)
            elif g > 0:
                pack_y_vector(g - 1, POOL_COLS, O)
            quantize_ao(2 * g + 3)
            if g > 0:
                quantize_y(g - 1, 0, O)
                store_words(g - 1, 0, O)
            if g < last - 1:
                quantize_ao(2 * g + 4)
        store_scales(0, EARLY_SCALE_GROUPS, [nc.sync, nc.sync])

        pack_y_pool(last - 1, 0, POOL_COLS_LATE)
        multiply_half(2 * last)
        spare = [turn_banks[i][:].rearrange("p a r -> p (a r)") for i in range(PACK)]
        for j in range(2):
            for t in range(2, PACK):
                multiply(last, t, j * HALF, (j + 1) * HALF, spare[2 * j + t - 2])
                weigh(last, t, j * HALF, (j + 1) * HALF)
        store_y(last, 2, PACK)
        pack_y_scalar(last - 1, POOL_COLS_LATE, O)
        pack_y_scalar(last, 0, HALF)
        pack_y_vector(last, HALF, O)
        quantize_y(last - 1, 0, O)
        store_words(last - 1, 0, O)
        quantize_y(last, HALF, O)
        store_words(last, HALF, O)
        quantize_y(last, 0, HALF)
        store_words(last, 0, HALF)
        store_scales(EARLY_SCALE_GROUPS, GROUPS, [nc.scalar, nc.sync])
